import numpy as np, ml_dtypes
CORES = [113,118,241,246]
N = 4
BF = ml_dtypes.bfloat16
W, L, S, T, F = 2048, 256, 1, 5, 256
C = W >> S
LEVELS = np.array([800, 900, 1000, 1050, 1100, 1150, 1250, 1400])
def parts(rng):
    d = {"key": rng.integers(0, 256, (N, 8, 16, W)), "em": rng.integers(0, 256, (N, 8, 16, W)), "cl": rng.integers(0, W, (N, 8, 16, C)), "pl": rng.integers(0, W, (N, 8, 16, L)),
         "q": rng.integers(0, 256, (N, 8, 16, L)), "emb": rng.integers(0, 256, (N, 8, 16, 16)), "w": rng.integers(0, 256, (N, 8, 16, 1))}
    base = np.stack([rng.permutation(LEVELS) for r in range(N)]).reshape(N, 8, 1, 1)
    d["th"] = base + rng.integers(-100, 101, (N, 8, 16, 1))
    return d
def pack(d):
    kinds = {"key": BF, "em": BF, "cl": np.int32, "pl": np.int32, "q": BF, "emb": BF, "w": BF, "th": np.float32}
    return {k: np.ascontiguousarray(d[k].reshape(N, 128, -1)).astype(np.float32).astype(t) for k, t in kinds.items()}
def setup_inputs(rng):
    return pack(parts(rng))
def setup_inputs_ties(rng):
    d = parts(rng); o = rng.permutation(8)
    for k in ("key", "q", "emb"): d[k] = 64 * rng.integers(0, 4, d[k].shape)
    d["th"] = 64 * rng.integers(16, 23, (N, 8, 16, 1)) + rng.integers(0, 2, (N, 8, 16, 1))
    d["em"] = rng.integers(0, 2, (N, 8, 16, W)) * rng.choice(np.array([1, 3, 255]), (N, 8, 1, 1))
    d["em"][:, o[0]] = 7; d["em"][:, o[1]] = 0
    for k in ("key", "q", "emb"):
        d[k][:, o[2]] = 0
        d[k][:, o[3]] = rng.integers(0, 32, d[k][:, o[3]].shape)
    d["th"][:, o[2], :, 0] = rng.permutation(np.arange(16) % 3)
    d["th"][:, o[3]] = rng.integers(1, 256, (N, 16, 1))
    return pack(d)
def setup_inputs_ends(rng):
    d = parts(rng); o = rng.permutation(8); ends = np.array([0, 1, W - 2, W - 1])
    d["pl"][:, o[0]] = rng.choice(ends, (N, 16, L)); d["th"][:, o[0]] = 4096
    d["th"][:, o[1]] = 0
    d["pl"][:, o[2]] = rng.integers(0, W, (N, 1, L))
    d["cl"][:, o[3]] = rng.choice(ends, (N, 16, C)); d["th"][:, o[3]] = 1000
    d["cl"][:, o[4]] = rng.integers(0, W, (N, 1, C))
    d["key"][:, o[5]] = d["key"][:, o[5]][:, :, :1]
    d["pl"][:, o[6]] = rng.choice(ends, (N, 16, L))
    d["th"][:, o[7]] = 0; d["w"][:, o[7]] = 0
    return pack(d)
def setup_inputs_lone(rng):
    d = parts(rng); d["th"] = np.zeros((N, 8, 16, 1), np.int64)
    for r in range(N):
        o = rng.permutation(8)
        d["th"][r, o[1], 0] = 4096; d["th"][r, o[2], 15] = 4096; d["th"][r, o[3], 14:] = 4096
        for g in o[4:]: d["th"][r, g, rng.integers(1, 15)] = 4096
    d["th"][rng.integers(0, N)] = 0
    return pack(d)
def setup_inputs_big(rng):
    d = parts(rng); o = rng.permutation(8)
    for k in ("key", "em", "q", "emb"): d[k] = 255 * rng.integers(0, 2, d[k].shape)
    d["w"] = rng.integers(254, 256, d["w"].shape)
    d["th"] = rng.choice(np.array([1785, 1786, 2040, 2041, 2295, 1020, 4080, 4081]), (N, 8, 16, 1))
    d["key"][:, o[0]] = 0; d["q"][:, o[0]] = 255; d["emb"][:, o[0]] = 255; d["w"][:, o[0]] = 255
    d["th"][:, o[0], :, 0] = 4080 + np.arange(16) % 2
    d["em"][:, o[1]] = 255
    d["th"][:, o[2]] = 0
    d["th"][:, o[3]] = 0; d["q"][:, o[3]] = 255; d["emb"][:, o[3]] = 255; d["w"][:, o[3]] = 255
    d["em"][:, o[4]] = 255 - (rng.random((N, 16, W)) < 0.0625)
    return pack(d)
def setup_inputs_spread(rng):
    d = parts(rng)
    for k in ("key", "em", "q", "emb"):
        s = d[k].shape
        d[k] = np.minimum((np.exp2(10 * rng.random(s[:2] + (1, s[3]))) * rng.random(s)).astype(np.int64), 255)
    d["w"] = np.minimum(np.exp2(8 * rng.random(d["w"].shape)).astype(np.int64), 255)
    d["th"] = np.minimum(np.exp2(8 + 4 * rng.random((N, 8, 16, 1))).astype(np.int64), 4096)
    for k in ("pl", "cl"): d[k] = np.minimum((W * rng.random(d[k].shape) ** 3).astype(np.int64), W - 1)
    return pack(d)
def check_inputs(d):
    bad = []
    for k, hi in (("key", 255), ("em", 255), ("cl", W - 1), ("pl", W - 1), ("q", 255), ("emb", 255), ("w", 255), ("th", 4096)):
        a = np.asarray(d[k]).astype(np.float64)
        if not np.all((a >= 0) & (a <= hi) & (a == np.floor(a))): bad.append("whole numbers and range of " + k)
    return bad
def reference(key, em, cl, pl, q, emb, w, th):
    def ints(a): return a.astype(np.float32).astype(np.int32).reshape(N, 8, 16, -1)
    K, E, CL, B, H, TH = ints(key), ints(em), ints(cl), ints(emb), ints(w), ints(th)
    p, x = ints(pl), ints(q)
    toks = [[] for r in range(N)]
    for t in range(T):
        pn, xn = [], []
        for r in range(N):
            at = np.take_along_axis(K[r], p[r].reshape(8, 1, 16 * L), 2).reshape(8, 16, 16, L)
            dist = np.add.reduce(np.abs(at - x[r][:, :, None, :]), axis=1)
            near = dist < TH[r]
            first = np.argmax(near, axis=1)
            lead = np.take_along_axis(p[r], first[:, None, :], 1)[:, 0]
            h = np.add.reduce(H[r] * x[r], axis=1)
            c = np.where(np.any(near, axis=1), lead >> S, h & (C - 1))
            pr = np.where(near, p[r], np.take_along_axis(CL[r], c[:, None, :], 2))
            v = np.add.reduce(np.take_along_axis(E[r], pr.reshape(8, 1, 16 * L), 2).reshape(8, 16, 16, L), axis=2)
            tok = np.argmax(v, axis=1)
            toks[r].append(tok)
            xn.append((x[r] + np.take_along_axis(B[r], tok[:, :, None], 1).transpose(0, 2, 1)) >> 1); pn.append(pr)
        p = np.stack([np.concatenate([(pn[(r - 1) % N][..., :F] + (1 if r == 0 else 0)) & (W - 1), (pn[(r + 1) % N][..., F:] - (1 if r == N - 1 else 0)) & (W - 1)], axis=2) for r in range(N)])
        x = np.stack([np.concatenate([xn[(r - 1) % N][..., :F], xn[(r + 1) % N][..., F:]], axis=2) for r in range(N)])
    yt = np.stack([np.concatenate(a, axis=1) for a in toks])
    return {"yp": p.reshape(N, 128, L).astype(np.float32), "yq": x.reshape(N, 128, L).astype(np.float32).astype(BF), "yt": yt.astype(np.float32)}

from concourse.mybir import AluOpType, ActivationFunctionType
from concourse.bass import DstId, RemoteDMATransfer

NR, NB, LB, NT = 4, 4, 64, 5
NC = 2
GW = 1024 // NC
HOP = 40
LINK = 3200

SCRATCH = {
    "keyb": ("sbuf", [128, 2064], "bfloat16"), "keys": ("sbuf", [128, 2048], "bfloat16"),
    "emt": ("sbuf", [128, 2064], "bfloat16"), "clb": ("sbuf", [128, 1032], "int32"),
    "plb": ("sbuf", [128, 256], "int32"), "qb": ("sbuf", [128, 256], "bfloat16"),
    "wb": ("sbuf", [128, 1], "bfloat16"), "thf": ("sbuf", [128, 1], "float32"), "eb": ("sbuf", [128, 16], "bfloat16"),
    "LU": ("sbuf", [128, 1280], "uint16"), "LP": ("sbuf", [128, 1280], "float16"), "LX": ("sbuf", [128, 1280], "float16"),
    "SU": ("sbuf", [128, 1280], "uint16"), "SP": ("sbuf", [128, 1280], "float16"), "SX": ("sbuf", [128, 1280], "float16"),
    "SYP": ("sbuf", [128, 256], "float32"), "SYQ": ("sbuf", [128, 256], "bfloat16"),
    "FYP": ("sbuf", [128, 256], "float32"), "FYQ": ("sbuf", [128, 256], "bfloat16"),
    "ip": ("sbuf", [128, 256], "int32"), "iq": ("sbuf", [128, 256], "int32"),
    "ob": ("sbuf", [128, 128], "bfloat16"), "oh": ("sbuf", [128, 64], "float16"), "idb": ("sbuf", [128, 128], "bfloat16"),
    "idh": ("sbuf", [128, 128], "float16"), "bm": ("sbuf", [128, 128], "bfloat16"), "bm0": ("sbuf", [128, 128], "bfloat16"),
    "wd": ("sbuf", [128, 144], "bfloat16"), "ub": ("sbuf", [128, 128], "bfloat16"), "u2": ("sbuf", [128, 128], "bfloat16"),
    "q2": ("sbuf", [128, 128], "bfloat16"), "cnt": ("sbuf", [128, 128], "bfloat16"), "bn": ("sbuf", [128, 128], "bfloat16"),
    "nk": ("sbuf", [128, 128], "float16"), "n4": ("sbuf", [128, 128], "bfloat16"), "db": ("sbuf", [128, 128], "bfloat16"),
    "ii": ("sbuf", [128, 1], "int32"), "ik": ("sbuf", [128, 1], "int32"), "io16": ("sbuf", [128, 1], "int32"),
    "kc": ("sbuf", [128, 1], "float32"), "odd": ("sbuf", [128, 1], "float32"), "even": ("sbuf", [128, 1], "float32"),
    "vb": ("sbuf", [128, 1], "float32"), "ca0": ("sbuf", [128, 1], "float32"), "ca1": ("sbuf", [128, 1], "float32"),
    "m0": ("sbuf", [128, 1], "float32"), "thb": ("sbuf", [128, 1], "float32"), "ck": ("sbuf", [128, 1], "float32"),
    "cn": ("sbuf", [128, 1], "float32"),
    "zb": ("sbuf", [128, 512], "bfloat16"), "zm": ("sbuf", [128, 512], "float16"),
    "f10r": ("sbuf", [128, 128], "bfloat16"), "f01r": ("sbuf", [128, 128], "bfloat16"), "fx": ("sbuf", [128, 512], "bfloat16"),
    "sl": ("sbuf", [128, 128], "bfloat16"), "mk": ("sbuf", [128, 64], "float32"), "wt": ("sbuf", [128, 640], "float16"),
    "m2": ("sbuf", [128, 32], "float32"), "t2": ("sbuf", [128, 32], "float32"), "et": ("sbuf", [128, 16], "float32"),
    "tab": ("sbuf", [128, 80], "float32"),
    "toku": ("sbuf", [128, 80], "uint16"), "tokb": ("sbuf", [128, 80], "bfloat16"), "ytb": ("sbuf", [128, 1280], "float32"),
}
for _n, _s, _d in (("kk", [128, 256], "float16"), ("sg", [128, 256], "bfloat16"), ("nn", [128, 256], "bfloat16"),
                   ("y", [128, 16, 16], "float16"), ("zh", [128, 16, 16], "float16"), ("zt", [128, 16, 32], "float32"),
                   ("cc", [128, 16], "uint16"), ("cm", [128, 256], "float16"), ("vt", [128, 256], "float32"),
                   ("sc", [128, 256], "float32"), ("ti", [128, 16], "int32"), ("tv", [128, 16], "bfloat16")):
    SCRATCH[_n] = ("sbuf", _s, _d)
for _b in range(NB):
    SCRATCH.update({
        "xr%d" % _b: ("sbuf", [128, 1024], "float16"), "df%d" % _b: ("sbuf", [128, 1024], "bfloat16"),
        "ad%d" % _b: ("sbuf", [128, 1024], "bfloat16"), "eg%d" % _b: ("sbuf", [128, 1024], "bfloat16"),
        "pa%d" % _b: ("psum", [128, 16, 32], "float32"), "pb%d" % _b: ("psum", [128, 512], "float32"),
    })
LOADS = ["pl", "q", "key", "w", "th", "cl", "emb", "em", "keys"]
SEMAPHORES = (["cv", "cs", "ct", "cg", "sent"] + ["ld_" + n for n in LOADS]
              + ["ar%d_%d" % (t, b) for t in range(1, NT) for b in range(NB)]
              + ["ap%d" % b for b in range(NB)] + ["aq%d" % b for b in range(NB)]
              + ["op%d" % b for b in range(NB)] + ["oq%d" % b for b in range(NB)] + ["oy%d" % k for k in range(3)])


def rank_program(g, core, T, topo):
    rank = T.rank_of(core)
    if rank is None:
        return
    A, F = AluOpType, ActivationFunctionType
    V, S, P, Y = g.vector, g.scalar, g.tensor, g.sync
    nxt = T.cores[(rank + 1) % NR]
    rid, pid = topo.addr(nxt, core)
    eng = topo.engines(core, nxt)[:8]

    def mask(es):
        return sum(1 << e for e in es)

    o1 = 1 if rank == 0 else 0
    ops, seq = [], [0]

    def op(q, dur, emit, R=(), W=(), banks=(), sem=None, val=1, lat=0, skip=False, bias=0):
        ops.append({"q": q, "dur": dur, "emit": emit, "R": list(R), "W": list(W), "banks": list(banks), "sem": sem, "val": val,
                    "lat": lat, "skip": skip, "i": len(ops), "bias": bias - 4000 * seq[0]})

    def cyc(n):
        return max(64, n) + 4

    def load(q, name, fn, W, done, skip=False, bias=0):
        op(q, 80, fn, (), W, sem="ld_" + name, val=16, lat=done, skip=skip, bias=bias)

    load("Y", "pl", lambda: Y.dma_start(T.plb[:], T.pl[:]), ["plb"], 2300, bias=9e6)
    load("S", "q", lambda: S.dma_start(T.qb[:], T.q[:]), ["qb"], 2300, bias=9e6)
    load("Y", "key", lambda: Y.dma_start(T.keyb[:, 0:2048], T.key[:]), ["key"], 4600, bias=8e6)
    load("S", "w", lambda: S.dma_start(T.wb[:], T.w[:]), ["wb"], 2300, bias=8e6)
    load("S", "th", lambda: S.dma_start(T.thf[:], T.th[:]), ["thf"], 2300, bias=7e6)
    load("S", "emb", lambda: S.dma_start(T.eb[:], T.emb[:]), ["eb"], 2300, bias=6e6)
    load("Y", "cl", lambda: Y.dma_start(T.clb[:, 0:1024], T.cl[:]), ["cl"], 6900, bias=7e6)
    load("Y", "em", lambda: Y.dma_start(T.emt[:, 0:2048], T.em[:]), ["em"], 9000, bias=6e6)
    load("Y", "keys", lambda: Y.dma_start(T.keys[:, 0:2047], T.key[:, 1:2048]), ["keys"], 11000, skip=rank != 0, bias=5e6)

    op("V", cyc(256), lambda: V.tensor_copy(T.LU[:, 0:256], T.plb[:]), ["plb"], [("LU", 0, b) for b in range(NB)])
    op("V", cyc(128), lambda: V.tensor_copy(T.LX[:, 0:256], T.qb[:]), ["qb"], [("LX", 0, b) for b in range(NB)])
    op("V", cyc(256), lambda: V.tensor_copy(T.LP[:, 0:256], T.plb[:]), ["plb"], [("LP", 0, b) for b in range(NB)])
    op("V", 68, lambda: V.memset(T.ob[:], 1.0), (), ["ob"])

    def aff(out, src, pat, cmp, base, cm, n):
        op("G", 180 + 2 * n, lambda: g.affine_select(T[out][:], T[src][:], pat, cmp, 0.0, base, cm), [src], [out])

    aff("bm0", "ob", [[-16, 8], [0, 16]], A.is_ge, 0, 1, 128)
    aff("bm", "bm0", [[16, 8], [0, 16]], A.is_ge, 15, -1, 128)
    aff("idb", "ob", [[-1, 128]], A.is_equal, 0, 1, 128)
    op("G", 140, lambda: g.iota(T.ii[:], [[0, 1]], 0, 1), (), ["ii"])
    aff("ub", "bm", [[1, 128]], A.is_ge, -1, -1, 128)
    aff("f10r", "ob", [[1, 128]], A.is_equal, -16, -1, 128)
    aff("f01r", "ob", [[1, 128]], A.is_equal, 16, -1, 128)
    aff("sl", "ob", [[-1, 16], [-16, 8]], A.is_equal, 0, 1, 128)

    def ts(out, i, s1, s2, a, b, R, W, n=1):
        if b is None:
            op("V", cyc(n), lambda: V.tensor_scalar(out, i, s1, None, a), R, W)
        else:
            op("V", cyc(n), lambda: V.tensor_scalar(out, i, s1, s2, a, b), R, W)

    def cp(out, i, R, W, n=1):
        op("V", cyc(n), lambda: V.tensor_copy(out, i), R, W)

    op("V", 76, lambda: V.memset(T.wd[:], 0.0), (), ["wd"])
    cp(T.wd[:, 15:128:16], T.bm[:, 0::16], ["bm"], ["wd"])
    ts(T.ik[:], T.ii[:], 15, None, A.bitwise_and, None, ["ii"], ["ik"])
    ts(T.io16[:], T.ii[:], 16, None, A.bitwise_and, None, ["ii"], ["io16"])
    cp(T.kc[:], T.ik[:], ["ik"], ["kc"])
    ts(T.odd[:], T.io16[:], 0.0625, None, A.mult, None, ["io16"], ["odd"])
    ts(T.even[:], T.odd[:], -1.0, 1.0, A.mult, A.add, ["odd"], ["even"])
    ts(T.thb[:], T.thf[:], -0.5, None, A.add, None, ["thf"], ["thb"])
    cp(T.idh[:], T.idb[:], ["idb"], ["idh"], 64)
    ts(T.u2[:], T.ub[:], -2048.0, None, A.mult, None, ["ub"], ["u2"], 64)
    ts(T.q2[:], T.idb[:], 2048.0, None, A.mult, None, ["idb"], ["q2"], 64)
    op("V", 260, lambda: V.tensor_tensor(T.cnt[:], T.u2[:], T.q2[:], A.add), ["u2", "q2"], ["cnt"])
    ts(T.bn[:], T.bm[:], -2048.0, None, A.mult, None, ["bm"], ["bn"], 64)
    ts(T.nk[:], T.idb[:], -2048.0, None, A.mult, None, ["idb"], ["nk"], 64)
    ts(T.n4[:], T.idb[:], -4096.0, None, A.mult, None, ["idb"], ["n4"], 64)
    for t in range(NT):
        ts(T.wt[:, 128 * t:128 * t + 128], T.bm[:], T.wb[:], 2.0 ** (1 - t), A.mult, A.mult, ["bm", "wb"], [("wt", t)], 64)
    op("P", 64, lambda: P.matmul(T.pb0[:, 511:512], T.bm[:], T.wb[:], True, True), ["bm", "wb"], ["sw"], banks=["b0"])
    op("V", 68, lambda: V.tensor_scalar(T.ck[:], T.pb0[:, 511:512], -1.0, 1025.0 - 511.5 / 1024, A.mult, A.add), ["sw"], ["ck"],
       banks=["b0"])
    op("V", 68, lambda: V.tensor_scalar(T.cn[:], T.pb0[:, 511:512], -2048.0, float(2048 * 1025 + 2 - 32768), A.mult, A.add),
       ["sw"], ["cn"], banks=["b0"])
    ts(T.ca0[:], T.kc[:], -2048.0, -2046.0, A.mult, A.add, ["kc"], ["ca0"])
    op("V", 68, lambda: V.memset(T.zb[:], 0.0), (), ["zb"])
    cp(T.zb[:, 0:128:32], T.bm[:, 0::32], ["bm"], ["zb"])
    cp(T.zb[:, 128:256:32], T.bm[:, 16::32], ["bm"], ["zb"])
    ts(T.m0[:], T.kc[:], 0.0, None, A.is_equal, None, ["kc"], ["m0"])
    ts(T.zb[:, 256:384:32], T.bm[:, 0::32], T.m0[:], None, A.mult, None, ["bm", "m0"], ["zb"])
    ts(T.zb[:, 384:512:32], T.bm[:, 16::32], T.m0[:], None, A.mult, None, ["bm", "m0"], ["zb"])
    cp(T.zm[:], T.zb[:], ["zb"], ["zm"], 256)
    cp(T.oh[:], T.ob[:, 0:64], ["ob"], ["oh"])
    ts(T.vb[:], T.kc[:], -0.0625, 0.46875, A.mult, A.add, ["kc"], ["vb"])
    ts(T.db[:], T.idb[:], T.vb[:], None, A.mult, None, ["idb", "vb"], ["db"], 64)
    op("V", 68, lambda: V.memset(T.mk[:], 1.0), (), ["mk"])
    op("V", 68, lambda: V.memset(T.mk[:, 0::16], 0.0), (), ["mk"])
    fsrc = [("idb", "even"), ("f01r", "odd"), ("f10r", "even"), ("idb", "odd")]
    for j, (m, c) in enumerate(fsrc):
        ts(T.fx[:, 128 * j:128 * j + 128], T[m][:], T[c][:], None, A.mult, None, [m, c], [("fx", j)], 64)
    ts(T.m2[:, 0:16], T.eb[:], T.even[:], None, A.mult, None, ["eb", "even"], ["m2"])
    ts(T.m2[:, 16:32], T.eb[:], T.odd[:], None, A.mult, None, ["eb", "odd"], ["m2b"])
    op("V", 68, lambda: V.transpose(T.t2[:], T.m2[:]), ["m2", "m2b"], ["t2"])
    op("V", 68, lambda: V.tensor_tensor(T.et[:], T.t2[:, 0:16], T.t2[:, 16:32], A.add), ["t2"], ["et"])
    for t in range(NT):
        ts(T.tab[:, 16 * t:16 * t + 16], T.et[:], 2047.5 if t == 0 else 1023.5, 2.0 ** t, A.add, A.mult, ["et"], [("tab", t)])
    ts(T.ca1[:], T.kc[:], -2048.0, -2046.0 + o1, A.mult, A.add, ["kc"], ["ca1"])
    cp(T.clb[:, 1024:1025], T.clb[:, 0:1], ["cl"], ["clx"])
    op("S", 80, lambda: S.activation(T.emt[:, 2048:2049], T.emt[:, 0:1], F.Copy), ["em"], ["emx"])
    op("S", 80, lambda: S.activation(T.keyb[:, 2048:2049], T.keyb[:, 0:1], F.Copy), ["key"], ["keyx"])
    op("S", 80, lambda: S.activation(T.keys[:, 2047:2048], T.keyb[:, 0:1], F.Copy), ["key", "keys"], ["keysx"], skip=rank != 0)

    def group(ms):
        def f():
            last = None
            for m in ms:
                last = P.matmul(*m)
            return last
        return f

    def arrive(t, b):
        return "ar%d_%d" % (t, b)

    def yt_out(k, ts_):
        n = len(ts_)
        lo, hi = ts_[0], ts_[-1] + 1
        cp(T.tokb[:, 16 * lo:16 * hi], T.toku[:, 16 * lo:16 * hi], [("tok", t, b) for t in ts_ for b in range(NB)], [("tokb", k)])
        bk, lastb = T["pa%d" % (NB - 1)], NB - 1
        op("P", 16 * 64, group([(bk[0:8, 0:8 * n, j::16], T.sl[:, 8 * j:8 * j + 8], T.tokb[:, 16 * lo:16 * hi], True, True)
                                for j in range(16)]), ["sl", ("tokb", k)], ["ytp"] + [(x, lastb) for x in ("D", "Q", "Z", "TK")],
           banks=["a%d" % lastb])
        op("S", 80 + 256 * n, lambda: S.activation(T.ytb[0:8, 256 * lo:256 * hi], bk[0:8, 0:8 * n, :], F.Copy), ["ytp"],
           [("ytb", k)], banks=["a%d" % lastb])
        op("Y", 80, lambda: Y.dma_start(T.yt[:, 256 * lo:256 * hi], T.ytb[0:8, 256 * lo:256 * hi]), [("ytb", k)], (),
           sem="oy%d" % k, val=16, lat=2200)

    for t in range(NT):
        for b in range(NB):
            c0 = 256 * t + LB * b
            seq[0] = t * NB + b
            cs = slice(c0, c0 + LB)
            bA, bB = "a%d" % b, "b%d" % b
            pa, pb = T["pa%d" % b], T["pb%d" % b]
            D, Q, Z, TK = pa[:, 4:6, :], pa[:, 6:8, :], pa[:, 0:4, :], pa[:, 8, 0:4]
            H, PA, PN, VT = pb[:, 0:64], pb[:, 64:128], pb[:, 128:192], pb[:, 192:256]
            xr, df, ad, eg = T["xr%d" % b], T["df%d" % b], T["ad%d" % b], T["eg%d" % b]
            bl, b4 = slice(LB * b, LB * b + LB), slice(4 * b, 4 * b + 4)
            kk, sg, nn, cm, vt, sc = [T[n][:, bl] for n in ("kk", "sg", "nn", "cm", "vt", "sc")]
            y, zh, zt = [T[n][:, b4, :] for n in ("y", "zh", "zt")]
            cc, ti, tv = [T[n][:, b4] for n in ("cc", "ti", "tv")]
            shifted = rank == 0 and t > 0
            if t:
                op("N", 0, None, [("snd", t - 1, b)], [(n, t, b) for n in ("LU", "LP", "LX")], sem=arrive(t, b), val=8)
            LU, LP, LX = T.LU[:, cs], T.LP[:, cs], T.LX[:, cs]
            wt = T.wt[:, 128 * t:128 * t + 128]
            if t:
                op("V", cyc(32), lambda xr=xr, LX=LX, t=t: V.tensor_scalar(xr[:, 0::16], LX, 2.0 ** -t, -1024.0, A.mult, A.add),
                   [("LX", t, b)], [("xr", b, j) for j in range(2)])
            else:
                op("V", cyc(32), lambda xr=xr, LX=LX: V.tensor_copy(xr[:, 0::16], LX), [("LX", t, b)],
                   [("xr", b, j) for j in range(2)])
            for st in (8, 4, 2):
                op("V", cyc(256 // st), lambda xr=xr, st=st: V.tensor_copy(xr[:, st::2 * st], xr[:, 0::2 * st]), [("xr", b, 0)],
                   [("xr", b, 0)])
            op("V", cyc(256), lambda xr=xr: V.tensor_copy(xr[:, 1::2], xr[:, 0::2]), [("xr", b, 0)], [("xr", b, 1)])
            for h in range(NC):
                e = slice(GW * h, GW * h + GW)
                win = T.keys[:, 0:2048] if shifted else T.keyb[:, 0:2049] if t else T.keyb[:, 0:2048]
                off = T.LU[:, c0 + GW // 16 * h:c0 + GW // 16 * (h + 1)]
                op("V", 60 + 1.6 * GW, lambda df=df, xr=xr, e=e, win=win, off=off: V.tensor_tensor(df[:, e], win.indirect(off),
                                                                                                   xr[:, e], A.subtract),
                   (["keys", "keysx"] if shifted else ["key", "keyx"] if t else ["key"])
                   + [("LU", t, b), ("xr", b, 0), ("xr", b, 1)], [("df", b, h)])
                op("S", 70 + GW, lambda df=df, ad=ad, e=e: S.activation(ad[:, e], df[:, e], F.Abs), [("df", b, h)], [("ad", b, h)])
                if h == 0:
                    op("P", 64, group([(H, wt, LX, True, True)]), [("LX", t, b), ("wt", t)], [("H", b)], banks=[bB])
                    op("V", 68, lambda kk=kk, H=H, t=t: V.tensor_scalar(kk, H, 2.0 ** -11, T.ck[:] if t else 1025.0 - 511.5 / 1024,
                                                                        A.mult, A.add), [("H", b), "ck"], [("kk", b)], banks=[bB])
            op("P", 1024, group([(D, T.wd[:, 15 - i:143 - i], ad[:, i::16], i == 0, i == 15) for i in range(16)]),
               [("ad", b, h) for h in range(NC)] + ["wd"], [("D", b)], banks=[bA])
            op("S", 140, lambda sg=sg, D=D: S.activation(sg, D, F.Sign, bias=T.thb[:], scale=-1.0), [("D", b), "thb"],
               [("sg", b)], banks=[bA])
            op("P", 320, group([(PA, T.idh[:], LP, True, False), (PA, T.cnt[:], sg, False, True),
                                (PN, wt, LX, True, False), (PN, T.nk[:], kk, False, False), (PN, T.bn[:], sg, False, True)]),
               [("LP", t, b), ("LX", t, b), ("wt", t), ("kk", b), ("sg", b), "idh", "cnt", "nk", "bn"], [("AN", b)], banks=[bB])
            op("S", 140, lambda sg=sg, nn=nn: S.activation(nn, sg, F.Relu, scale=-1.0), [("sg", b)], [("nn", b)])
            op("V", 68, lambda y=y, PA=PA, t=t: V.tensor_scalar(y, PA, T.ca1[:] if t else T.ca0[:], 0.0, A.add, A.max),
               [("AN", b), "ca1", "ca0"], [("y", b)], banks=[bB])
            op("V", 68, lambda zh=zh, PN=PN, t=t: V.tensor_scalar(zh, PN, T.cn[:] if t else float(2048 * 1025 + 2 - 32768), 0.0,
                                                                  A.add, A.max), [("AN", b), "cn"], [("zh", b)], banks=[bB])
            zm = T.zm
            op("P", 256, group([(Z[:, :, 0:16], zm[:, 0:128], y, True, False), (Z[:, :, 0:16], zm[:, 256:384], zh, False, True),
                                (Z[:, :, 16:32], zm[:, 128:256], y, True, False),
                                (Z[:, :, 16:32], zm[:, 384:512], zh, False, True)]),
               [("y", b), ("zh", b), "zm"], [("Z", b)], banks=[bA])
            op("V", cyc(128), lambda zt=zt, Z=Z: V.transpose(zt, Z), [("Z", b)], [("zt", b)], banks=[bA])
            op("P", 128 + 64 * (t > 0), group([(Q, T.idh[:], LP, True, False)]
                                              + ([(Q, T.idh[:], T.oh[:], False, False)] if shifted else [])
                                              + [(Q, T.n4[:], nn, False, True)]),
               [("LP", t, b), ("nn", b), "idh", "oh", "n4"], [("Q", b)], banks=[bA])
            op("V", 68, lambda cc=cc, zt=zt: V.tensor_scalar(cc, zt[:, :, 0], 0.5, -1.25, A.mult, A.add), [("zt", b)], [("cc", b)])
            clw = T.clb[:, 0:1025] if t else T.clb[:, 0:1024]
            op("V", 170, lambda cm=cm, cc=cc, nn=nn, clw=clw: V.tensor_tensor(cm, clw.indirect(cc), nn, A.mult),
               [("cc", b), ("nn", b), "cl"] + (["clx"] if t else []), [("cm", b)])
            SP, SU, SX = T.SP[:, cs], T.SU[:, cs], T.SX[:, cs]
            op("V", 68, lambda SP=SP, cm=cm, Q=Q: V.tensor_tensor(SP, cm, Q, A.max), [("cm", b), ("Q", b)], [("SP", t, b)],
               banks=[bA])
            op("V", 68, lambda SU=SU, SP=SP: V.tensor_copy(SU, SP), [("SP", t, b)], [("SU", t, b)])
            emw = T.emt[:, 0:2049] if t else T.emt[:, 0:2048]
            for h in range(NC):
                e = slice(GW * h, GW * h + GW)
                off = T.SU[:, c0 + GW // 16 * h:c0 + GW // 16 * (h + 1)]
                op("S", 80 + 1.6 * GW, lambda eg=eg, e=e, emw=emw, off=off: S.activation(eg[:, e], emw.indirect(off), F.Copy),
                   [("SU", t, b), "em"] + (["emx"] if t else []), [("eg", b, h)])
            if t == NT - 1:
                ts(T.ip[:, bl], SP, 1.0 if rank == NR - 1 else 0.0, None, A.add, None, [("SP", t, b)], [("ip", b)], 64)
                ts(T.iq[:, bl], T.ip[:, bl], 2047, None, A.bitwise_and, None, [("ip", b)], [("iq", b)], 64)
                cp(T.SYP[:, bl], T.iq[:, bl], [("iq", b)], [("SYP", b)], 64)
                op("G", 900, lambda b=b, bl=bl: g.remote_dma(T.FYP[:, bl], T.SYP[:, bl], T.sem["ap%d" % b], T.sem.sent, pid, rid,
                                                             mask(eng)), [("SYP", b)], [("fp", b)], sem="sent", val=len(eng))
                op("N", 0, None, [("fp", b)], [("FYP", b)], sem="ap%d" % b, val=8)
                op("Y", 80, lambda b=b, bl=bl: Y.dma_start(T.yp[:, bl], T.FYP[:, bl]), [("FYP", b)], (), sem="op%d" % b, val=16,
                   lat=2200)
            op("P", 17 * 64, group([(VT, T.db[:], T.ob[:, 0:64], True, False)]
                                   + [(VT, T.idb[:], eg[:, i::16], False, i == 15) for i in range(16)]),
               [("eg", b, h) for h in range(NC)] + ["db", "ob", "idb"], [("VT", b)], banks=[bB])
            op("V", 68, lambda vt=vt, VT=VT: V.transpose(vt, VT), [("VT", b)], [("vt", b)], banks=[bB])
            op("V", 68, lambda vt=vt, sc=sc: V.tensor_tensor_scan(sc, T.mk[:], vt, 0.0, A.mult, A.max), [("vt", b), "mk"],
               [("sc", b)])
            op("V", 68, lambda ti=ti, sc=sc: V.tensor_copy(ti, sc[:, 15::16]), [("sc", b)], [("ti", b)])
            op("V", 68, lambda tv=tv, ti=ti, sc=sc: V.tensor_tensor(tv, sc[:, 15::16], ti, A.subtract), [("sc", b), ("ti", b)],
               [("tv", b)])
            op("P", 256, group([(TK[:, hf::2], T.fx[:, 256 * e + 128 * hf:256 * e + 128 * hf + 128], tv[:, e::2], e == 0, e == 1)
                                for hf in range(2) for e in range(2)]), [("tv", b)] + [("fx", j) for j in range(4)], [("TK", b)],
               banks=[bA])
            tok = T.toku[:, 16 * t + 4 * b:16 * t + 4 * b + 4]
            op("V", 68, lambda tok=tok, TK=TK: V.tensor_scalar(tok, TK, -16.0, 7.5, A.mult, A.add), [("TK", b)], [("tok", t, b)],
               banks=[bA])
            op("V", 170, lambda SX=SX, tok=tok, LX=LX, t=t: V.tensor_tensor(SX, T.tab[:, 16 * t:16 * t + 16].indirect(tok), LX, A.add),
               [("tok", t, b), ("LX", t, b), ("tab", t)], [("SX", t, b)])
            if t < NT - 1:
                d0 = 256 * (t + 1) + LB * b
                ds = slice(d0, d0 + LB)

                def send(ds=ds, SU=SU, SP=SP, SX=SX, t=t, b=b):
                    dst, sem = [DstId(rid=rid, pnc=pid)], T.sem[arrive(t + 1, b)]
                    return g.remote_dma_fused([
                        RemoteDMATransfer(dst_ids=dst, dma_engine_mask=mask(es), remote_sem=sem, src=a, dst=d)
                        for es, a, d in ((eng[0:2], SU, T.LU[:, ds]), (eng[2:4], SP, T.LP[:, ds]), (eng[4:8], SX, T.LX[:, ds]))],
                        local_sem=T.sem.sent)
                op("G", 900, send, [("SU", t, b), ("SP", t, b), ("SX", t, b)], [("snd", t, b)], sem="sent", val=len(eng))
            else:
                ts(T.SYQ[:, bl], SX, 2.0 ** -NT, -1024.0, A.mult, A.add, [("SX", t, b)], [("SYQ", b)], 32)
                op("G", 900, lambda b=b, bl=bl: g.remote_dma(T.FYQ[:, bl], T.SYQ[:, bl], T.sem["aq%d" % b], T.sem.sent, pid, rid,
                                                             mask(eng)), [("SYQ", b)], [("fq", b)], sem="sent", val=len(eng))
                op("N", 0, None, [("fq", b)], [("FYQ", b)], sem="aq%d" % b, val=8)
                op("Y", 80, lambda b=b, bl=bl: Y.dma_start(T.yq[:, bl], T.FYQ[:, bl]), [("FYQ", b)], (), sem="oq%d" % b, val=16,
                   lat=2200)
        if t == 1:
            yt_out(0, [0, 1])
        if t == 3:
            yt_out(1, [2, 3])
    yt_out(2, [4])

    schedule(ops)
    emit_all(ops, {"V": V, "S": S, "P": P, "G": g, "Y": Y}, T, g)


CNT_SEM = {"V": "cv", "S": "cs", "P": "ct", "G": "cg"}


def schedule(ops):
    lastw, readers, bank = {}, {}, {}
    for o in ops:
        d = set()
        for k in o["R"]:
            if k in lastw:
                d.add(lastw[k])
            readers.setdefault(k, []).append(o["i"])
        for k in o["W"]:
            if k in lastw:
                d.add(lastw[k])
            d.update(readers.get(k, []))
            lastw[k], readers[k] = o["i"], []
        for k in o["banks"]:
            for q, i in bank.setdefault(k, [])[-40:]:
                if q != o["q"]:
                    d.add(i)
            bank[k].append((o["q"], o["i"]))
        d.discard(o["i"])
        o["D"] = d
    n = len(ops)
    succ = [[] for _ in range(n)]
    for o in ops:
        for d in o["D"]:
            succ[d].append(o["i"])
    tail = [0.0] * n
    for o in reversed(ops):
        w = max([tail[s] for s in succ[o["i"]]] + [0])
        tail[o["i"]] = w + o["dur"] + o["lat"] + (LINK if o["q"] == "N" else HOP)
    free = {q: 0.0 for q in "VSPGYN"}
    left = [len(o["D"]) for o in ops]
    ready = {q: [] for q in "VSPGYN"}
    avail = [0.0] * n
    for o in ops:
        if not left[o["i"]]:
            ready[o["q"]].append(o["i"])
    done = 0
    while done < n:
        best = None
        for q in "VSPGYN":
            if not ready[q]:
                continue
            if q == "N":
                i = min(ready[q], key=lambda j: avail[j])
                st = avail[i]
            else:
                st = max(free[q], min(avail[j] for j in ready[q]))
                i = max((j for j in ready[q] if avail[j] <= st + 1e-9), key=lambda j: tail[j] + ops[j]["bias"])
            if best is None or st < best[0]:
                best = (st, q, i)
        st, q, i = best
        o = ops[i]
        ready[q].remove(i)
        o["st"] = st
        end = st + o["dur"]
        if q != "N":
            free[q] = end
        fin = end + o["lat"] + (LINK if q == "N" else HOP)
        o["end"] = fin
        done += 1
        for s in succ[i]:
            avail[s] = max(avail[s], fin)
            left[s] -= 1
            if not left[s]:
                ready[ops[s]["q"]].append(s)


def emit_all(ops, queues, T, g):
    order = sorted((o for o in ops if not o["skip"]), key=lambda o: (o["st"], o["i"]))
    count, known, total, clock = {}, {q: {} for q in "VSPGYN"}, {}, {}
    for o in order:
        q = o["q"]
        kn = known[q]
        if q == "N":
            clock[o["i"]] = {o["sem"]: o["val"]}
            total[o["sem"]] = o["val"]
            o["tok"] = (o["sem"], o["val"])
            continue
        eng = queues[q]
        for d in sorted((ops[i] for i in o["D"]), key=lambda x: -x["end"]):
            if d["skip"]:
                continue
            s, v = d["tok"]
            if kn.get(s, 0) >= v:
                continue
            eng.wait_ge(T.sem[s], v)
            for a, w in clock[d["i"]].items():
                if kn.get(a, 0) < w:
                    kn[a] = w
        ins = o["emit"]()
        if o["sem"] == "sent":
            total["sent"] = total.get("sent", 0) + o["val"]
            o["tok"] = ("sent", 0)
            clock[o["i"]] = {}
            continue
        if o["sem"] is not None:
            ins.then_inc(T.sem[o["sem"]], o["val"])
            s, v = o["sem"], o["val"]
        else:
            s = CNT_SEM[q]
            count[s] = count.get(s, 0) + 1
            v = count[s]
            ins.then_inc(T.sem[s], 1)
        total[s] = v
        o["tok"] = (s, v)
        ck = dict(kn)
        ck[s] = v
        clock[o["i"]] = ck
    for s, v in sorted(total.items()):
        g.wait_ge(T.sem[s], v)
